import numpy as np, ml_dtypes
CORES = [8,136,40,168]
N = 4
C = 64
SIGN = [[1,1,1,1],[1,-1,1,-1],[1,1,-1,-1],[1,-1,-1,1]]
def setup_inputs(rng):
    return {"x": rng.standard_normal((N, 128, C), dtype=np.float32).astype(ml_dtypes.bfloat16)}
def setup_inputs_big(rng):
    d = setup_inputs(rng)
    for k in ("x",): d[k] = (d[k].astype(np.float32) * 1048576.0).astype(d[k].dtype)
    return d
def setup_inputs_small(rng):
    d = setup_inputs(rng)
    for k in ("x",): d[k] = (d[k].astype(np.float32) * (1 / 1048576.0)).astype(d[k].dtype)
    return d
def setup_inputs_apart(rng):
    d = setup_inputs(rng)
    f = (10.0 ** rng.permutation(np.linspace(-1.5, 1.5, N))).astype(np.float32).reshape(N, 1, 1)
    for k in ("x",): d[k] = (d[k].astype(np.float32) * f).astype(d[k].dtype)
    return d
def reference(x):
    X = x.astype(np.float64)
    y = np.stack([sum(SIGN[r][j] * X[j] for j in range(N)) for r in range(N)])
    return {"y": y.astype(ml_dtypes.bfloat16)}

@@ -1,0 +1,64 @@
+from concourse.bass import DstId, RemoteDMATransfer
+from concourse.mybir import AluOpType
+
+SCRATCH = {
+    "xd": ("dram", [128, 64], "bfloat16"),
+    "buf": ("sbuf", [128, 256], "bfloat16"),
+    "u": ("sbuf", [128, 128], "float32"),
+    "ysb": ("sbuf", [128, 64], "bfloat16"),
+}
+SEMAPHORES = ["staged", "own", "arrived", "half", "done", "stored"]
+
+
+def rank_program(g, core, T, topo):
+    r = T.rank_of(core)
+    if r is None:
+        return
+    cores = T.cores
+    n = len(cores)
+    c = T.x.shape[1]
+    s = T.tables["SIGN"][r]
+    sem = T.sem
+
+    def slot(j):
+        return T.buf[:, j * c:(j + 1) * c]
+
+    g.sync.dma_start(T.xd[:, :], T.x[:, :]).then_inc(sem.staged, 16)
+    g.sync.dma_start(slot(r), T.x[:, :]).then_inc(sem.own, 16)
+
+    peers = [cores[r ^ k] for k in range(1, n)]
+    mask = topo.mask(core, peers[0])
+    for d in peers:
+        assert topo.may_write(core, d) and topo.same_plane(core, d)
+        mask &= topo.mask(core, d)
+    engines = bin(mask).count("1")
+    ids = []
+    for d in peers:
+        rid, pid = topo.addr(d, core)
+        ids.append(DstId(rid=rid, pnc=pid))
+    g.wait_ge(sem.staged, 16)
+    g.remote_dma_fused(
+        [RemoteDMATransfer(dst_ids=ids, dma_engine_mask=mask, remote_sem=sem.arrived,
+                           srcs=[T.xd[:, :]], dsts=[slot(r) for _ in peers], alu_op=0)],
+        local_sem=sem.arrived)
+
+    h = n // 2
+    assert n == 4 and s[0] * s[h] == s[1] * s[h + 1]
+    op1 = AluOpType.add if s[0] == s[h] else AluOpType.subtract
+    v = g.vector
+    v.wait_ge(sem.own, 16)
+    v.wait_ge(sem.arrived, engines * n)
+    v.tensor_tensor(T.u[:, :], T.buf[:, 0:h * c], T.buf[:, h * c:n * c], op1).then_inc(sem.half, 1)
+    v.wait_ge(sem.half, 1)
+    u0, u1 = T.u[:, 0:c], T.u[:, c:2 * c]
+    assert s[0] > 0 or s[1] > 0
+    if s[0] == s[1]:
+        v.tensor_tensor(T.ysb[:, :], u0, u1, AluOpType.add).then_inc(sem.done, 1)
+    elif s[0] > 0:
+        v.tensor_tensor(T.ysb[:, :], u0, u1, AluOpType.subtract).then_inc(sem.done, 1)
+    else:
+        v.tensor_tensor(T.ysb[:, :], u1, u0, AluOpType.subtract).then_inc(sem.done, 1)
+
+    g.sync.wait_ge(sem.done, 1)
+    g.sync.dma_start(T.y[:, :], T.ysb[:, :]).then_inc(sem.stored, 16)
+    g.sync.wait_ge(sem.stored, 16)

@@ -4,10 +4,13 @@ from concourse.mybir import AluOpType
 SCRATCH = {
     "xd": ("dram", [128, 64], "bfloat16"),
     "buf": ("sbuf", [128, 256], "bfloat16"),
-    "u": ("sbuf", [128, 128], "float32"),
+    "dif": ("sbuf", [128, 128], "bfloat16"),
+    "wp": ("sbuf", [128, 128], "bfloat16"),
+    "wm": ("sbuf", [128, 128], "bfloat16"),
+    "acc": ("psum", [128, 64], "float32"),
     "ysb": ("sbuf", [128, 64], "bfloat16"),
 }
-SEMAPHORES = ["staged", "own", "arrived", "half", "done", "stored"]
+SEMAPHORES = ["staged", "own", "from0", "from1", "from2", "from3", "sent", "ramp", "wts", "part", "done", "stored"]
 
 
 def rank_program(g, core, T, topo):
@@ -26,7 +29,8 @@ def rank_program(g, core, T, topo):
     g.sync.dma_start(T.xd[:, :], T.x[:, :]).then_inc(sem.staged, 16)
     g.sync.dma_start(slot(r), T.x[:, :]).then_inc(sem.own, 16)
 
-    peers = [cores[r ^ k] for k in range(1, n)]
+    order = [r ^ k for k in range(1, n)]
+    peers = [cores[j] for j in order]
     mask = topo.mask(core, peers[0])
     for d in peers:
         assert topo.may_write(core, d) and topo.same_plane(core, d)
@@ -38,27 +42,38 @@ def rank_program(g, core, T, topo):
         ids.append(DstId(rid=rid, pnc=pid))
     g.wait_ge(sem.staged, 16)
     g.remote_dma_fused(
-        [RemoteDMATransfer(dst_ids=ids, dma_engine_mask=mask, remote_sem=sem.arrived,
+        [RemoteDMATransfer(dst_ids=ids, dma_engine_mask=mask, remote_sem=sem["from%d" % r],
                            srcs=[T.xd[:, :]], dsts=[slot(r) for _ in peers], alu_op=0)],
-        local_sem=sem.arrived)
+        local_sem=sem.sent)
 
-    h = n // 2
-    assert n == 4 and s[0] * s[h] == s[1] * s[h + 1]
-    op1 = AluOpType.add if s[0] == s[h] else AluOpType.subtract
+    early = [r] + order[:-1]
+    last = order[-1]
+    g.iota(T.dif[:, :], [[-1, 128]], 0, 1, allow_small_or_imprecise_dtypes=True).then_inc(sem.ramp, 1)
     v = g.vector
-    v.wait_ge(sem.own, 16)
-    v.wait_ge(sem.arrived, engines * n)
-    v.tensor_tensor(T.u[:, :], T.buf[:, 0:h * c], T.buf[:, h * c:n * c], op1).then_inc(sem.half, 1)
-    v.wait_ge(sem.half, 1)
-    u0, u1 = T.u[:, 0:c], T.u[:, c:2 * c]
-    assert s[0] > 0 or s[1] > 0
-    if s[0] == s[1]:
-        v.tensor_tensor(T.ysb[:, :], u0, u1, AluOpType.add).then_inc(sem.done, 1)
-    elif s[0] > 0:
-        v.tensor_tensor(T.ysb[:, :], u0, u1, AluOpType.subtract).then_inc(sem.done, 1)
-    else:
-        v.tensor_tensor(T.ysb[:, :], u1, u0, AluOpType.subtract).then_inc(sem.done, 1)
+    v.wait_ge(sem.ramp, 1)
+    made = 0
+    for sign, w in ((1, T.wp), (-1, T.wm)):
+        if any(s[j] == sign for j in early):
+            v.tensor_scalar(w[:, :], T.dif[:, :], 0.0, float(sign), AluOpType.is_equal, AluOpType.mult).then_inc(sem.wts, 1)
+            made += 1
+
+    pe = g.tensor
+    pe.wait_ge(sem.wts, made)
+    for i, j in enumerate(early):
+        if j == r:
+            pe.wait_ge(sem.own, 16)
+        else:
+            pe.wait_ge(sem["from%d" % j], engines)
+        w = T.wp if s[j] > 0 else T.wm
+        mm = pe.matmul(T.acc[:, :], w[:, :], slot(j), i == 0, i == len(early) - 1)
+    mm.then_inc(sem.part, 1)
+
+    v.wait_ge(sem.part, 1)
+    v.wait_ge(sem["from%d" % last], engines)
+    op = AluOpType.add if s[last] > 0 else AluOpType.subtract
+    v.tensor_tensor(T.ysb[:, :], T.acc[:, :], slot(last), op).then_inc(sem.done, 1)
 
     g.sync.wait_ge(sem.done, 1)
     g.sync.dma_start(T.y[:, :], T.ysb[:, :]).then_inc(sem.stored, 16)
+    g.wait_ge(sem.sent, engines)
     g.sync.wait_ge(sem.stored, 16)

from concourse.bass import DstId, RemoteDMATransfer
from concourse.mybir import AluOpType

SCRATCH = {
    "xd": ("dram", [128, 64], "bfloat16"),
    "buf": ("sbuf", [128, 256], "bfloat16"),
    "dif": ("sbuf", [128, 128], "bfloat16"),
    "wp": ("sbuf", [128, 128], "bfloat16"),
    "wm": ("sbuf", [128, 128], "bfloat16"),
    "acc": ("psum", [128, 64], "float32"),
    "ysb": ("sbuf", [128, 64], "bfloat16"),
}
SEMAPHORES = ["staged", "own", "from0", "from1", "from2", "from3", "sent", "ramp", "wts", "part", "done", "stored"]


def rank_program(g, core, T, topo):
    r = T.rank_of(core)
    if r is None:
        return
    cores = T.cores
    n = len(cores)
    c = T.x.shape[1]
    s = T.tables["SIGN"][r]
    sem = T.sem

    def slot(j):
        return T.buf[:, j * c:(j + 1) * c]

    g.sync.dma_start(T.xd[:, :], T.x[:, :]).then_inc(sem.staged, 16)
    g.sync.dma_start(slot(r), T.x[:, :]).then_inc(sem.own, 16)

    order = [r ^ k for k in range(1, n)]
    peers = [cores[j] for j in order]
    mask = topo.mask(core, peers[0])
    for d in peers:
        assert topo.may_write(core, d) and topo.same_plane(core, d)
        mask &= topo.mask(core, d)
    engines = bin(mask).count("1")
    ids = []
    for d in peers:
        rid, pid = topo.addr(d, core)
        ids.append(DstId(rid=rid, pnc=pid))
    g.wait_ge(sem.staged, 16)
    g.remote_dma_fused(
        [RemoteDMATransfer(dst_ids=ids, dma_engine_mask=mask, remote_sem=sem["from%d" % r],
                           srcs=[T.xd[:, :]], dsts=[slot(r) for _ in peers], alu_op=0)],
        local_sem=sem.sent)

    early = [r] + order[:-1]
    last = order[-1]
    g.iota(T.dif[:, :], [[-1, 128]], 0, 1, allow_small_or_imprecise_dtypes=True).then_inc(sem.ramp, 1)
    v = g.vector
    v.wait_ge(sem.ramp, 1)
    made = 0
    for sign, w in ((1, T.wp), (-1, T.wm)):
        if any(s[j] == sign for j in early):
            v.tensor_scalar(w[:, :], T.dif[:, :], 0.0, float(sign), AluOpType.is_equal, AluOpType.mult).then_inc(sem.wts, 1)
            made += 1

    pe = g.tensor
    pe.wait_ge(sem.wts, made)
    for i, j in enumerate(early):
        if j == r:
            pe.wait_ge(sem.own, 16)
        else:
            pe.wait_ge(sem["from%d" % j], engines)
        w = T.wp if s[j] > 0 else T.wm
        mm = pe.matmul(T.acc[:, :], w[:, :], slot(j), i == 0, i == len(early) - 1)
    mm.then_inc(sem.part, 1)

    v.wait_ge(sem.part, 1)
    v.wait_ge(sem["from%d" % last], engines)
    op = AluOpType.add if s[last] > 0 else AluOpType.subtract
    v.tensor_tensor(T.ysb[:, :], T.acc[:, :], slot(last), op).then_inc(sem.done, 1)

    g.sync.wait_ge(sem.done, 1)
    g.sync.dma_start(T.y[:, :], T.ysb[:, :]).then_inc(sem.stored, 16)
    g.wait_ge(sem.sent, engines)
    g.sync.wait_ge(sem.stored, 16)
